import numpy as np, ml_dtypes
CORES = [50,51,58,59,102,103,110,111]
N = 8
G1 = [0,1,2,3,4,5,6,7]
G2 = [0,1,2,3]
G3 = [4,5,6,7]
ROOT3 = 0
def setup_inputs(rng):
    return {"x1": rng.standard_normal((N, 128, 512), dtype=np.float32), "x2": rng.standard_normal((N, 128, 16), dtype=np.float32).astype(ml_dtypes.bfloat16), "x3": rng.standard_normal((N, 128, 32), dtype=np.float32)}
def reference(x1, x2, x3):
    out = {}
    y = np.full((N, 128, 512), np.nan, x1.dtype)
    for i, r in enumerate(G1):
        y[r] = np.concatenate([x1[s][:, 64 * i:64 * i + 64] for s in G1], axis=1)
    out["y1"] = y
    y = np.full((N, 128, 16), np.nan, x2.dtype)
    s = x2[G2].sum(axis=0, dtype=np.float64).astype(x2.dtype)
    for r in G2:
        y[r] = s
    out["y2"] = y
    y = np.full((N, 128, 32), np.nan, x3.dtype)
    for r in G3:
        y[r] = x3[G3[ROOT3]]
    out["y3"] = y
    return out

@@ -1,0 +1,159 @@
+from concourse.bass import DstId, RemoteDMATransfer
+
+SCRATCH = {
+    "snd": ("sbuf", [128, 512], "float32"),
+    "land": ("sbuf", [128, 512], "float32"),
+    "hbuf": ("sbuf", [128, 128], "float32"),
+    "a2src": ("dram", [128, 16], "bfloat16"),
+    "a2land": ("dram", [4, 128, 16], "bfloat16"),
+    "a2res": ("dram", [128, 16], "bfloat16"),
+    "b3": ("dram", [128, 32], "float32"),
+}
+SEMAPHORES = ["lfar", "lnear", "lsm", "farr", "narr", "harr", "a2arr", "a2done", "b3arr", "sent", "st1", "st2"]
+
+FORWARD = False
+B = 64
+
+
+def _dst(topo, c):
+    rid, pid, _ = topo.addr(c)
+    return DstId(rid=rid, pnc=pid)
+
+
+def _fold_core(chip):
+    return chip * 8 + (4 if FORWARD else 0)
+
+
+def _fwd_cores(c):
+    k = c % 8
+    base = c - k
+    return base + ((k + 4) % 8), base + k - 2
+
+
+def rank_program(g, core, T, topo):
+    cores = list(T.cores)
+    G1 = [cores[r] for r in T.tables["G1"]]
+    G2 = [cores[r] for r in T.tables["G2"]]
+    G3 = [cores[r] for r in T.tables["G3"]]
+    root3 = G3[T.tables["ROOT3"]]
+    S = T.sem
+    chip = topo.chip
+
+    fold_chips = sorted(set(chip(c) for c in G2))
+    if core in [_fold_core(ch) for ch in fold_chips]:
+        mine = [c for c in G2 if chip(c) == chip(core)]
+        g.wait_ge(S.a2arr, 8 * len(G2))
+        masks = [0x00FF, 0xFF00]
+        g.remote_dma_fused(
+            [RemoteDMATransfer(dst_ids=[_dst(topo, c)], dma_engine_mask=masks[k], remote_sem=S.a2done,
+                               srcs=[T.a2land[m] for m in range(len(G2))], dsts=[T.a2res[:]], alu_op=1)
+             for k, c in enumerate(mine)], local_sem=S.sent)
+        g.wait_ge(S.sent, 8 * len(mine))
+        return
+
+    if FORWARD:
+        for i, c in enumerate(G1):
+            p, q = _fwd_cores(c)
+            if core in (p, q):
+                far = [j for j, d in enumerate(G1) if chip(d) // 2 != chip(c) // 2]
+                same = (core == q)
+                tg = [j for j in far if ((chip(G1[j]) & 1) == (chip(c) & 1)) == same]
+                g.wait_ge(S.harr, 8)
+                g.remote_dma_fused(
+                    [RemoteDMATransfer(dst_ids=[_dst(topo, G1[j])], dma_engine_mask=(0x0F, 0xF0)[k],
+                                       remote_sem=S.farr, src=T.hbuf[:, B * k:B * k + B],
+                                       dst=T.land[:, B * i:B * i + B]) for k, j in enumerate(tg)],
+                    local_sem=S.sent)
+                g.wait_ge(S.sent, 8)
+                return
+
+    if core not in cores:
+        return
+
+    i = G1.index(core)
+    far = [j for j, d in enumerate(G1) if chip(d) // 2 != chip(core) // 2]
+    near = [j for j, d in enumerate(G1) if chip(d) // 2 == chip(core) // 2]
+    f0, f1 = B * far[0], B * far[-1] + B
+    n0, n1 = B * near[0], B * near[-1] + B
+    sent = 0
+
+    g.sync.dma_start(T.snd[:, f0:f1], T.x1[:, f0:f1]).then_inc(S.lfar, 16)
+    if core in G2:
+        g.scalar.dma_start(T.a2src[:], T.x2[:]).then_inc(S.lsm, 16)
+    if core == root3:
+        g.scalar.dma_start(T.b3[:], T.x3[:]).then_inc(S.lsm, 16)
+    g.scalar.dma_start(T.snd[:, n0:n1], T.x1[:, n0:n1]).then_inc(S.lnear, 16)
+    g.scalar.dma_start(T.land[:, B * i:B * i + B], T.x1[:, B * i:B * i + B]).then_inc(S.narr, 16)
+
+    if core in G2:
+        m = G2.index(core)
+        g.wait_ge(S.lsm, 16)
+        g.remote_dma_fused(
+            [RemoteDMATransfer(dst_ids=[_dst(topo, _fold_core(ch))],
+                               dma_engine_mask=(0xFF00 if ch == chip(core) else 0x00FF),
+                               remote_sem=S.a2arr, src=T.a2src[:], dst=T.a2land[m]) for ch in fold_chips],
+            local_sem=S.sent)
+        sent += 8 * len(fold_chips)
+    if core == root3:
+        g.wait_ge(S.lsm, 16)
+        tr = []
+        off = [0x000F, 0x00F0]
+        for c in G3:
+            if c == core:
+                continue
+            mk = 0xFF00 if chip(c) == chip(core) else off.pop(0)
+            tr.append(RemoteDMATransfer(dst_ids=[_dst(topo, c)], dma_engine_mask=mk, remote_sem=S.b3arr,
+                                        src=T.b3[:], dst=T.b3[:]))
+        g.remote_dma_fused(tr, local_sem=S.sent)
+        sent += 16
+
+    g.wait_ge(S.lfar, 16)
+    if FORWARD:
+        p, q = _fwd_cores(core)
+        diag = [j for j in far if (chip(G1[j]) & 1) != (chip(core) & 1)]
+        same = [j for j in far if (chip(G1[j]) & 1) == (chip(core) & 1)]
+        g.remote_dma_fused(
+            [RemoteDMATransfer(dst_ids=[_dst(topo, h)], dma_engine_mask=mk, remote_sem=S.harr,
+                               src=T.snd[:, B * js[0]:B * js[-1] + B], dst=T.hbuf[:])
+             for h, js, mk in ((p, diag, 0x00FF), (q, same, 0xFF00))], local_sem=S.sent)
+        sent += 16
+        far_total = 4 * len(far)
+    else:
+        g.remote_dma_fused(
+            [RemoteDMATransfer(dst_ids=[_dst(topo, G1[j])], dma_engine_mask=0x3 << (2 * k), remote_sem=S.farr,
+                               src=T.snd[:, B * j:B * j + B], dst=T.land[:, B * i:B * i + B])
+             for k, j in enumerate(far)], local_sem=S.sent)
+        sent += 8
+        far_total = 2 * len(far)
+
+    g.wait_ge(S.lnear, 16)
+    tr = []
+    off = [0x000F, 0x00F0]
+    for j in near:
+        if j == i:
+            continue
+        mk = 0xFF00 if chip(G1[j]) == chip(core) else off.pop(0)
+        tr.append(RemoteDMATransfer(dst_ids=[_dst(topo, G1[j])], dma_engine_mask=mk, remote_sem=S.narr,
+                                    src=T.snd[:, B * j:B * j + B], dst=T.land[:, B * i:B * i + B]))
+    g.remote_dma_fused(tr, local_sem=S.sent)
+    sent += 16
+
+    g.sync.wait_ge(S.farr, far_total)
+    g.sync.dma_start(T.y1[:, f0:f1], T.land[:, f0:f1]).then_inc(S.st1, 16)
+    g.sync.wait_ge(S.narr, 32)
+    g.sync.dma_start(T.y1[:, n0:n1], T.land[:, n0:n1]).then_inc(S.st1, 16)
+    g.sync.wait_ge(S.st1, 32)
+
+    if core in G2:
+        g.scalar.wait_ge(S.a2done, 8)
+        g.scalar.dma_start(T.y2[:], T.a2res[:]).then_inc(S.st2, 16)
+        g.scalar.wait_ge(S.st2, 16)
+    if core in G3:
+        if core == root3:
+            g.scalar.dma_start(T.y3[:], T.x3[:]).then_inc(S.st2, 16)
+        else:
+            g.scalar.wait_ge(S.b3arr, 8 if chip(core) == chip(root3) else 4)
+            g.scalar.dma_start(T.y3[:], T.b3[:]).then_inc(S.st2, 16)
+        g.scalar.wait_ge(S.st2, 16)
+
+    g.wait_ge(S.sent, sent)

@@ -11,7 +11,7 @@ SCRATCH = {
 }
 SEMAPHORES = ["lfar", "lnear", "lsm", "farr", "narr", "harr", "a2arr", "a2done", "b3arr", "sent", "st1", "st2"]
 
-FORWARD = False
+FORWARD = True
 B = 64
 
 

@@ -11,7 +11,6 @@ SCRATCH = {
 }
 SEMAPHORES = ["lfar", "lnear", "lsm", "farr", "narr", "harr", "a2arr", "a2done", "b3arr", "sent", "st1", "st2"]
 
-FORWARD = True
 B = 64
 
 
@@ -21,7 +20,7 @@ def _dst(topo, c):
 
 
 def _fold_core(chip):
-    return chip * 8 + (4 if FORWARD else 0)
+    return chip * 8 + 4
 
 
 def _fwd_cores(c):
@@ -51,21 +50,20 @@ def rank_program(g, core, T, topo):
         g.wait_ge(S.sent, 8 * len(mine))
         return
 
-    if FORWARD:
-        for i, c in enumerate(G1):
-            p, q = _fwd_cores(c)
-            if core in (p, q):
-                far = [j for j, d in enumerate(G1) if chip(d) // 2 != chip(c) // 2]
-                same = (core == q)
-                tg = [j for j in far if ((chip(G1[j]) & 1) == (chip(c) & 1)) == same]
-                g.wait_ge(S.harr, 8)
-                g.remote_dma_fused(
-                    [RemoteDMATransfer(dst_ids=[_dst(topo, G1[j])], dma_engine_mask=(0x0F, 0xF0)[k],
-                                       remote_sem=S.farr, src=T.hbuf[:, B * k:B * k + B],
-                                       dst=T.land[:, B * i:B * i + B]) for k, j in enumerate(tg)],
-                    local_sem=S.sent)
-                g.wait_ge(S.sent, 8)
-                return
+    for i, c in enumerate(G1):
+        p, q = _fwd_cores(c)
+        if core in (p, q):
+            far = [j for j, d in enumerate(G1) if chip(d) // 2 != chip(c) // 2]
+            same = (core == q)
+            tg = [j for j in far if ((chip(G1[j]) & 1) == (chip(c) & 1)) == same]
+            g.wait_ge(S.harr, 8)
+            g.remote_dma_fused(
+                [RemoteDMATransfer(dst_ids=[_dst(topo, G1[j])], dma_engine_mask=(0x0F, 0xF0)[k],
+                                   remote_sem=S.farr, src=T.hbuf[:, B * k:B * k + B],
+                                   dst=T.land[:, B * i:B * i + B]) for k, j in enumerate(tg)],
+                local_sem=S.sent)
+            g.wait_ge(S.sent, 8)
+            return
 
     if core not in cores:
         return
@@ -108,23 +106,14 @@ def rank_program(g, core, T, topo):
         sent += 16
 
     g.wait_ge(S.lfar, 16)
-    if FORWARD:
-        p, q = _fwd_cores(core)
-        diag = [j for j in far if (chip(G1[j]) & 1) != (chip(core) & 1)]
-        same = [j for j in far if (chip(G1[j]) & 1) == (chip(core) & 1)]
-        g.remote_dma_fused(
-            [RemoteDMATransfer(dst_ids=[_dst(topo, h)], dma_engine_mask=mk, remote_sem=S.harr,
-                               src=T.snd[:, B * js[0]:B * js[-1] + B], dst=T.hbuf[:])
-             for h, js, mk in ((p, diag, 0x00FF), (q, same, 0xFF00))], local_sem=S.sent)
-        sent += 16
-        far_total = 4 * len(far)
-    else:
-        g.remote_dma_fused(
-            [RemoteDMATransfer(dst_ids=[_dst(topo, G1[j])], dma_engine_mask=0x3 << (2 * k), remote_sem=S.farr,
-                               src=T.snd[:, B * j:B * j + B], dst=T.land[:, B * i:B * i + B])
-             for k, j in enumerate(far)], local_sem=S.sent)
-        sent += 8
-        far_total = 2 * len(far)
+    p, q = _fwd_cores(core)
+    diag = [j for j in far if (chip(G1[j]) & 1) != (chip(core) & 1)]
+    same = [j for j in far if (chip(G1[j]) & 1) == (chip(core) & 1)]
+    g.remote_dma_fused(
+        [RemoteDMATransfer(dst_ids=[_dst(topo, h)], dma_engine_mask=mk, remote_sem=S.harr,
+                           src=T.snd[:, B * js[0]:B * js[-1] + B], dst=T.hbuf[:])
+         for h, js, mk in ((p, diag, 0x00FF), (q, same, 0xFF00))], local_sem=S.sent)
+    sent += 16
 
     g.wait_ge(S.lnear, 16)
     tr = []
@@ -138,22 +127,21 @@ def rank_program(g, core, T, topo):
     g.remote_dma_fused(tr, local_sem=S.sent)
     sent += 16
 
-    g.sync.wait_ge(S.farr, far_total)
+    g.sync.wait_ge(S.farr, 4 * len(far))
     g.sync.dma_start(T.y1[:, f0:f1], T.land[:, f0:f1]).then_inc(S.st1, 16)
-    g.sync.wait_ge(S.narr, 32)
-    g.sync.dma_start(T.y1[:, n0:n1], T.land[:, n0:n1]).then_inc(S.st1, 16)
-    g.sync.wait_ge(S.st1, 32)
+    g.sync.wait_ge(S.st1, 16)
 
     if core in G2:
         g.scalar.wait_ge(S.a2done, 8)
         g.scalar.dma_start(T.y2[:], T.a2res[:]).then_inc(S.st2, 16)
-        g.scalar.wait_ge(S.st2, 16)
     if core in G3:
         if core == root3:
             g.scalar.dma_start(T.y3[:], T.x3[:]).then_inc(S.st2, 16)
         else:
             g.scalar.wait_ge(S.b3arr, 8 if chip(core) == chip(root3) else 4)
             g.scalar.dma_start(T.y3[:], T.b3[:]).then_inc(S.st2, 16)
-        g.scalar.wait_ge(S.st2, 16)
+    g.scalar.wait_ge(S.narr, 32)
+    g.scalar.dma_start(T.y1[:, n0:n1], T.land[:, n0:n1]).then_inc(S.st2, 16)
+    g.scalar.wait_ge(S.st2, 32)
 
     g.wait_ge(S.sent, sent)

@@ -9,7 +9,7 @@ SCRATCH = {
     "a2res": ("dram", [128, 16], "bfloat16"),
     "b3": ("dram", [128, 32], "float32"),
 }
-SEMAPHORES = ["lfar", "lnear", "lsm", "farr", "narr", "harr", "a2arr", "a2done", "b3arr", "sent", "st1", "st2"]
+SEMAPHORES = ["lfar", "lnear", "lsm", "fsam", "fdia", "narr", "harr", "a2arr", "a2done", "b3arr", "sent", "st1", "st2"]
 
 B = 64
 
@@ -59,7 +59,7 @@ def rank_program(g, core, T, topo):
             g.wait_ge(S.harr, 8)
             g.remote_dma_fused(
                 [RemoteDMATransfer(dst_ids=[_dst(topo, G1[j])], dma_engine_mask=(0x0F, 0xF0)[k],
-                                   remote_sem=S.farr, src=T.hbuf[:, B * k:B * k + B],
+                                   remote_sem=(S.fsam if same else S.fdia), src=T.hbuf[:, B * k:B * k + B],
                                    dst=T.land[:, B * i:B * i + B]) for k, j in enumerate(tg)],
                 local_sem=S.sent)
             g.wait_ge(S.sent, 8)
@@ -83,6 +83,16 @@ def rank_program(g, core, T, topo):
     g.scalar.dma_start(T.snd[:, n0:n1], T.x1[:, n0:n1]).then_inc(S.lnear, 16)
     g.scalar.dma_start(T.land[:, B * i:B * i + B], T.x1[:, B * i:B * i + B]).then_inc(S.narr, 16)
 
+    g.wait_ge(S.lfar, 16)
+    p, q = _fwd_cores(core)
+    diag = [j for j in far if (chip(G1[j]) & 1) != (chip(core) & 1)]
+    same = [j for j in far if (chip(G1[j]) & 1) == (chip(core) & 1)]
+    g.remote_dma_fused(
+        [RemoteDMATransfer(dst_ids=[_dst(topo, h)], dma_engine_mask=mk, remote_sem=S.harr,
+                           src=T.snd[:, B * js[0]:B * js[-1] + B], dst=T.hbuf[:])
+         for h, js, mk in ((p, diag, 0x00FF), (q, same, 0xFF00))], local_sem=S.sent)
+    sent += 16
+
     if core in G2:
         m = G2.index(core)
         g.wait_ge(S.lsm, 16)
@@ -105,16 +115,6 @@ def rank_program(g, core, T, topo):
         g.remote_dma_fused(tr, local_sem=S.sent)
         sent += 16
 
-    g.wait_ge(S.lfar, 16)
-    p, q = _fwd_cores(core)
-    diag = [j for j in far if (chip(G1[j]) & 1) != (chip(core) & 1)]
-    same = [j for j in far if (chip(G1[j]) & 1) == (chip(core) & 1)]
-    g.remote_dma_fused(
-        [RemoteDMATransfer(dst_ids=[_dst(topo, h)], dma_engine_mask=mk, remote_sem=S.harr,
-                           src=T.snd[:, B * js[0]:B * js[-1] + B], dst=T.hbuf[:])
-         for h, js, mk in ((p, diag, 0x00FF), (q, same, 0xFF00))], local_sem=S.sent)
-    sent += 16
-
     g.wait_ge(S.lnear, 16)
     tr = []
     off = [0x000F, 0x00F0]
@@ -127,9 +127,10 @@ def rank_program(g, core, T, topo):
     g.remote_dma_fused(tr, local_sem=S.sent)
     sent += 16
 
-    g.sync.wait_ge(S.farr, 4 * len(far))
-    g.sync.dma_start(T.y1[:, f0:f1], T.land[:, f0:f1]).then_inc(S.st1, 16)
-    g.sync.wait_ge(S.st1, 16)
+    for js, sem in ((same, S.fsam), (diag, S.fdia)):
+        g.sync.wait_ge(sem, 4 * len(js))
+        g.sync.dma_start(T.y1[:, B * js[0]:B * js[-1] + B], T.land[:, B * js[0]:B * js[-1] + B]).then_inc(S.st1, 16)
+    g.sync.wait_ge(S.st1, 32)
 
     if core in G2:
         g.scalar.wait_ge(S.a2done, 8)

from concourse.bass import DstId, RemoteDMATransfer

SCRATCH = {
    "snd": ("sbuf", [128, 512], "float32"),
    "land": ("sbuf", [128, 512], "float32"),
    "hbuf": ("sbuf", [128, 128], "float32"),
    "a2src": ("dram", [128, 16], "bfloat16"),
    "a2land": ("dram", [4, 128, 16], "bfloat16"),
    "a2res": ("dram", [128, 16], "bfloat16"),
    "b3": ("dram", [128, 32], "float32"),
}
SEMAPHORES = ["lfar", "lnear", "lsm", "fsam", "fdia", "narr", "harr", "a2arr", "a2done", "b3arr", "sent", "st1", "st2"]

B = 64


def _dst(topo, c):
    rid, pid, _ = topo.addr(c)
    return DstId(rid=rid, pnc=pid)


def _fold_core(chip):
    return chip * 8 + 4


def _fwd_cores(c):
    k = c % 8
    base = c - k
    return base + ((k + 4) % 8), base + k - 2


def rank_program(g, core, T, topo):
    cores = list(T.cores)
    G1 = [cores[r] for r in T.tables["G1"]]
    G2 = [cores[r] for r in T.tables["G2"]]
    G3 = [cores[r] for r in T.tables["G3"]]
    root3 = G3[T.tables["ROOT3"]]
    S = T.sem
    chip = topo.chip

    fold_chips = sorted(set(chip(c) for c in G2))
    if core in [_fold_core(ch) for ch in fold_chips]:
        mine = [c for c in G2 if chip(c) == chip(core)]
        g.wait_ge(S.a2arr, 8 * len(G2))
        masks = [0x00FF, 0xFF00]
        g.remote_dma_fused(
            [RemoteDMATransfer(dst_ids=[_dst(topo, c)], dma_engine_mask=masks[k], remote_sem=S.a2done,
                               srcs=[T.a2land[m] for m in range(len(G2))], dsts=[T.a2res[:]], alu_op=1)
             for k, c in enumerate(mine)], local_sem=S.sent)
        g.wait_ge(S.sent, 8 * len(mine))
        return

    for i, c in enumerate(G1):
        p, q = _fwd_cores(c)
        if core in (p, q):
            far = [j for j, d in enumerate(G1) if chip(d) // 2 != chip(c) // 2]
            same = (core == q)
            tg = [j for j in far if ((chip(G1[j]) & 1) == (chip(c) & 1)) == same]
            g.wait_ge(S.harr, 8)
            g.remote_dma_fused(
                [RemoteDMATransfer(dst_ids=[_dst(topo, G1[j])], dma_engine_mask=(0x0F, 0xF0)[k],
                                   remote_sem=(S.fsam if same else S.fdia), src=T.hbuf[:, B * k:B * k + B],
                                   dst=T.land[:, B * i:B * i + B]) for k, j in enumerate(tg)],
                local_sem=S.sent)
            g.wait_ge(S.sent, 8)
            return

    if core not in cores:
        return

    i = G1.index(core)
    far = [j for j, d in enumerate(G1) if chip(d) // 2 != chip(core) // 2]
    near = [j for j, d in enumerate(G1) if chip(d) // 2 == chip(core) // 2]
    f0, f1 = B * far[0], B * far[-1] + B
    n0, n1 = B * near[0], B * near[-1] + B
    sent = 0

    g.sync.dma_start(T.snd[:, f0:f1], T.x1[:, f0:f1]).then_inc(S.lfar, 16)
    if core in G2:
        g.scalar.dma_start(T.a2src[:], T.x2[:]).then_inc(S.lsm, 16)
    if core == root3:
        g.scalar.dma_start(T.b3[:], T.x3[:]).then_inc(S.lsm, 16)
    g.scalar.dma_start(T.snd[:, n0:n1], T.x1[:, n0:n1]).then_inc(S.lnear, 16)
    g.scalar.dma_start(T.land[:, B * i:B * i + B], T.x1[:, B * i:B * i + B]).then_inc(S.narr, 16)

    g.wait_ge(S.lfar, 16)
    p, q = _fwd_cores(core)
    diag = [j for j in far if (chip(G1[j]) & 1) != (chip(core) & 1)]
    same = [j for j in far if (chip(G1[j]) & 1) == (chip(core) & 1)]
    g.remote_dma_fused(
        [RemoteDMATransfer(dst_ids=[_dst(topo, h)], dma_engine_mask=mk, remote_sem=S.harr,
                           src=T.snd[:, B * js[0]:B * js[-1] + B], dst=T.hbuf[:])
         for h, js, mk in ((p, diag, 0x00FF), (q, same, 0xFF00))], local_sem=S.sent)
    sent += 16

    if core in G2:
        m = G2.index(core)
        g.wait_ge(S.lsm, 16)
        g.remote_dma_fused(
            [RemoteDMATransfer(dst_ids=[_dst(topo, _fold_core(ch))],
                               dma_engine_mask=(0xFF00 if ch == chip(core) else 0x00FF),
                               remote_sem=S.a2arr, src=T.a2src[:], dst=T.a2land[m]) for ch in fold_chips],
            local_sem=S.sent)
        sent += 8 * len(fold_chips)
    if core == root3:
        g.wait_ge(S.lsm, 16)
        tr = []
        off = [0x000F, 0x00F0]
        for c in G3:
            if c == core:
                continue
            mk = 0xFF00 if chip(c) == chip(core) else off.pop(0)
            tr.append(RemoteDMATransfer(dst_ids=[_dst(topo, c)], dma_engine_mask=mk, remote_sem=S.b3arr,
                                        src=T.b3[:], dst=T.b3[:]))
        g.remote_dma_fused(tr, local_sem=S.sent)
        sent += 16

    g.wait_ge(S.lnear, 16)
    tr = []
    off = [0x000F, 0x00F0]
    for j in near:
        if j == i:
            continue
        mk = 0xFF00 if chip(G1[j]) == chip(core) else off.pop(0)
        tr.append(RemoteDMATransfer(dst_ids=[_dst(topo, G1[j])], dma_engine_mask=mk, remote_sem=S.narr,
                                    src=T.snd[:, B * j:B * j + B], dst=T.land[:, B * i:B * i + B]))
    g.remote_dma_fused(tr, local_sem=S.sent)
    sent += 16

    for js, sem in ((same, S.fsam), (diag, S.fdia)):
        g.sync.wait_ge(sem, 4 * len(js))
        g.sync.dma_start(T.y1[:, B * js[0]:B * js[-1] + B], T.land[:, B * js[0]:B * js[-1] + B]).then_inc(S.st1, 16)
    g.sync.wait_ge(S.st1, 32)

    if core in G2:
        g.scalar.wait_ge(S.a2done, 8)
        g.scalar.dma_start(T.y2[:], T.a2res[:]).then_inc(S.st2, 16)
    if core in G3:
        if core == root3:
            g.scalar.dma_start(T.y3[:], T.x3[:]).then_inc(S.st2, 16)
        else:
            g.scalar.wait_ge(S.b3arr, 8 if chip(core) == chip(root3) else 4)
            g.scalar.dma_start(T.y3[:], T.b3[:]).then_inc(S.st2, 16)
    g.scalar.wait_ge(S.narr, 32)
    g.scalar.dma_start(T.y1[:, n0:n1], T.land[:, n0:n1]).then_inc(S.st2, 16)
    g.scalar.wait_ge(S.st2, 32)

    g.wait_ge(S.sent, sent)
